import numpy as np
import ml_dtypes

BF16 = ml_dtypes.bfloat16


def bf(x):
    return np.asarray(x, np.float32).astype(BF16)


def f32(x):
    return np.asarray(x, np.float32)


def f64(x):
    return np.asarray(x).astype(np.float64)


def striped(idx):
    return np.tile(idx.reshape(-1, 16).T, (8, 1))


S, K, M, N, E, Q = 256, 512, 128, 512, 4, 128


def two_experts():
    first = np.random.permutation(S).reshape(E, S // E)
    return np.concatenate([np.random.permutation(np.concatenate([first[e], first[(e + 1) % E]])) for e in range(E)])


def setup_inputs():
    return {"table": bf(np.random.standard_normal((K, S))), "w": bf(np.random.standard_normal((E, K, M)) / np.sqrt(K)), "b": f32(0.5 * np.random.standard_normal((M, 1))), "offs": striped(two_experts())}


def reference(table, w, b, offs):
    idx = offs[:16].T.reshape(-1)
    x = f64(table)[:, idx]
    y = np.concatenate([f64(w)[e].T @ x[:, e * Q : (e + 1) * Q] for e in range(E)], axis=1)
    return np.maximum(y + f64(b), 0.0)

@@ -1,0 +1,56 @@
+import concourse.mybir as mybir
+
+BF16, F32, U16 = mybir.dt.bfloat16, mybir.dt.float32, mybir.dt.uint16
+ADD, MAX = mybir.AluOpType.add, mybir.AluOpType.max
+
+P = 128
+S = 256
+K = 512
+M = 128
+E = 4
+Q = 128
+N = E * Q
+KB = K // P
+QC = Q // 16
+
+FLOPS = 2 * K * M * N
+
+
+def tile_gather_matmul_kernel(tc, table, w, b, offs, out):
+    nc = tc.nc
+    with (
+        tc.tile_pool(name="held", bufs=1) as held,
+        tc.psum_pool(name="psum", bufs=1) as psum,
+    ):
+        offsets = held.tile([P, N // 16], U16, name="offsets")
+        nc.sync.dma_start(offsets[:], offs)
+
+        blocks = []
+        for kb in range(KB):
+            block = held.tile([P, S], BF16, name=f"block{kb}")
+            nc.sync.dma_start(block[:], table[kb * P : (kb + 1) * P, :])
+            blocks.append(block)
+
+        weights = []
+        for e in range(E):
+            expert_w = held.tile([P, KB, M], BF16, name=f"weights{e}")
+            nc.scalar.dma_start(expert_w[:], w[e].rearrange("(kb p) m -> p kb m", p=P))
+            weights.append(expert_w)
+
+        bias = held.tile([P, 1], F32, name="bias")
+        nc.gpsimd.dma_start(bias[:], b)
+
+        for e in range(E):
+            bank = psum.tile([P, Q], F32, name=f"bank{e}")
+            piece = offsets[:, e * QC : (e + 1) * QC]
+            for kb in range(KB):
+                nc.tensor.matmul(
+                    bank[:],
+                    weights[e][:, kb, :],
+                    blocks[kb][:].indirect(piece),
+                    start=(kb == 0),
+                    stop=(kb == KB - 1),
+                )
+            result = held.tile([P, Q], F32, name=f"result{e}")
+            nc.vector.tensor_scalar(result[:], bank[:], bias[:, 0:1], 0.0, op0=ADD, op1=MAX)
+            nc.sync.dma_start(out[:, e * Q : (e + 1) * Q], result[:])

@@ -13,6 +13,8 @@ N = E * Q
 KB = K // P
 QC = Q // 16
 
+WARM_MATMULS = 16
+
 FLOPS = 2 * K * M * N
 
 
@@ -31,14 +33,20 @@ def tile_gather_matmul_kernel(tc, table, w, b, offs, out):
             nc.sync.dma_start(block[:], table[kb * P : (kb + 1) * P, :])
             blocks.append(block)
 
+        zeros = held.tile([P, P], BF16, name="zeros")
+        nc.vector.memset(zeros[:], 0.0)
+        unread = psum.tile([P, P], F32, name="unread")
+        for i in range(WARM_MATMULS):
+            nc.tensor.matmul(unread[:], zeros[:], zeros[:], start=True, stop=True)
+
+        bias = held.tile([P, 1], F32, name="bias")
+        nc.sync.dma_start(bias[:], b)
+
         weights = []
         for e in range(E):
             expert_w = held.tile([P, KB, M], BF16, name=f"weights{e}")
             nc.scalar.dma_start(expert_w[:], w[e].rearrange("(kb p) m -> p kb m", p=P))
             weights.append(expert_w)
-
-        bias = held.tile([P, 1], F32, name="bias")
-        nc.gpsimd.dma_start(bias[:], b)
 
         for e in range(E):
             bank = psum.tile([P, Q], F32, name=f"bank{e}")

@@ -13,7 +13,7 @@ N = E * Q
 KB = K // P
 QC = Q // 16
 
-WARM_MATMULS = 16
+WARM_MATMULS = 14
 
 FLOPS = 2 * K * M * N
 
@@ -27,10 +27,12 @@ def tile_gather_matmul_kernel(tc, table, w, b, offs, out):
         offsets = held.tile([P, N // 16], U16, name="offsets")
         nc.sync.dma_start(offsets[:], offs)
 
+
+        table_blocks = table.rearrange("(p kb) s -> kb p s", kb=KB)
         blocks = []
         for kb in range(KB):
             block = held.tile([P, S], BF16, name=f"block{kb}")
-            nc.sync.dma_start(block[:], table[kb * P : (kb + 1) * P, :])
+            nc.sync.dma_start(block[:], table_blocks[kb])
             blocks.append(block)
 
         zeros = held.tile([P, P], BF16, name="zeros")
@@ -45,7 +47,7 @@ def tile_gather_matmul_kernel(tc, table, w, b, offs, out):
         weights = []
         for e in range(E):
             expert_w = held.tile([P, KB, M], BF16, name=f"weights{e}")
-            nc.scalar.dma_start(expert_w[:], w[e].rearrange("(kb p) m -> p kb m", p=P))
+            nc.scalar.dma_start(expert_w[:], w[e].rearrange("(p kb) m -> p kb m", kb=KB))
             weights.append(expert_w)
 
         for e in range(E):

@@ -24,31 +24,34 @@ def tile_gather_matmul_kernel(tc, table, w, b, offs, out):
         tc.tile_pool(name="held", bufs=1) as held,
         tc.psum_pool(name="psum", bufs=1) as psum,
     ):
-        offsets = held.tile([P, N // 16], U16, name="offsets")
-        nc.sync.dma_start(offsets[:], offs)
-
-
         table_blocks = table.rearrange("(p kb) s -> kb p s", kb=KB)
-        blocks = []
-        for kb in range(KB):
-            block = held.tile([P, S], BF16, name=f"block{kb}")
-            nc.sync.dma_start(block[:], table_blocks[kb])
-            blocks.append(block)
+        offsets = held.tile([P, N // 16], U16, name="offsets")
+        blocks = [held.tile([P, S], BF16, name=f"block{kb}") for kb in range(KB)]
+        weights = [held.tile([P, KB, M], BF16, name=f"weights{e}") for e in range(E)]
+        bias = held.tile([P, 1], F32, name="bias")
+
+        def load_block(queue, kb):
+            queue.dma_start(blocks[kb][:], table_blocks[kb])
+
+        def load_weights(queue, e):
+            queue.dma_start(weights[e][:], w[e].rearrange("(p kb) m -> p kb m", kb=KB))
+
+        nc.sync.dma_start(offsets[:], offs)
+        load_block(nc.sync, 0)
+        load_weights(nc.scalar, 0)
+        load_block(nc.sync, 1)
+        load_block(nc.scalar, 2)
+        load_block(nc.scalar, 3)
+        load_weights(nc.sync, 1)
+        load_weights(nc.scalar, 2)
+        nc.sync.dma_start(bias[:], b)
+        load_weights(nc.sync, 3)
 
         zeros = held.tile([P, P], BF16, name="zeros")
         nc.vector.memset(zeros[:], 0.0)
         unread = psum.tile([P, P], F32, name="unread")
         for i in range(WARM_MATMULS):
             nc.tensor.matmul(unread[:], zeros[:], zeros[:], start=True, stop=True)
-
-        bias = held.tile([P, 1], F32, name="bias")
-        nc.sync.dma_start(bias[:], b)
-
-        weights = []
-        for e in range(E):
-            expert_w = held.tile([P, KB, M], BF16, name=f"weights{e}")
-            nc.scalar.dma_start(expert_w[:], w[e].rearrange("(p kb) m -> p kb m", kb=KB))
-            weights.append(expert_w)
 
         for e in range(E):
             bank = psum.tile([P, Q], F32, name=f"bank{e}")

@@ -38,13 +38,13 @@ def tile_gather_matmul_kernel(tc, table, w, b, offs, out):
 
         nc.sync.dma_start(offsets[:], offs)
         load_block(nc.sync, 0)
-        load_weights(nc.scalar, 0)
+        load_weights(nc.sync, 0)
         load_block(nc.sync, 1)
-        load_block(nc.scalar, 2)
-        load_block(nc.scalar, 3)
+        load_block(nc.sync, 2)
+        load_block(nc.sync, 3)
         load_weights(nc.sync, 1)
-        load_weights(nc.scalar, 2)
         nc.sync.dma_start(bias[:], b)
+        load_weights(nc.sync, 2)
         load_weights(nc.sync, 3)
 
         zeros = held.tile([P, P], BF16, name="zeros")

@@ -43,9 +43,9 @@ def tile_gather_matmul_kernel(tc, table, w, b, offs, out):
         load_block(nc.sync, 2)
         load_block(nc.sync, 3)
         load_weights(nc.sync, 1)
-        nc.sync.dma_start(bias[:], b)
         load_weights(nc.sync, 2)
         load_weights(nc.sync, 3)
+        nc.sync.dma_start(bias[:], b)
 
         zeros = held.tile([P, P], BF16, name="zeros")
         nc.vector.memset(zeros[:], 0.0)

@@ -36,13 +36,15 @@ def tile_gather_matmul_kernel(tc, table, w, b, offs, out):
         def load_weights(queue, e):
             queue.dma_start(weights[e][:], w[e].rearrange("(p kb) m -> p kb m", kb=KB))
 
+        turns = ((0, 1), (2,), (3,))
+
         nc.sync.dma_start(offsets[:], offs)
         load_block(nc.sync, 0)
         load_weights(nc.sync, 0)
+        load_weights(nc.sync, 1)
         load_block(nc.sync, 1)
         load_block(nc.sync, 2)
         load_block(nc.sync, 3)
-        load_weights(nc.sync, 1)
         load_weights(nc.sync, 2)
         load_weights(nc.sync, 3)
         nc.sync.dma_start(bias[:], b)
@@ -53,17 +55,18 @@ def tile_gather_matmul_kernel(tc, table, w, b, offs, out):
         for i in range(WARM_MATMULS):
             nc.tensor.matmul(unread[:], zeros[:], zeros[:], start=True, stop=True)
 
-        for e in range(E):
-            bank = psum.tile([P, Q], F32, name=f"bank{e}")
-            piece = offsets[:, e * QC : (e + 1) * QC]
+        banks = [psum.tile([P, Q], F32, name=f"bank{e}") for e in range(E)]
+        for turn in turns:
             for kb in range(KB):
-                nc.tensor.matmul(
-                    bank[:],
-                    weights[e][:, kb, :],
-                    blocks[kb][:].indirect(piece),
-                    start=(kb == 0),
-                    stop=(kb == KB - 1),
-                )
-            result = held.tile([P, Q], F32, name=f"result{e}")
-            nc.vector.tensor_scalar(result[:], bank[:], bias[:, 0:1], 0.0, op0=ADD, op1=MAX)
-            nc.sync.dma_start(out[:, e * Q : (e + 1) * Q], result[:])
+                for e in turn:
+                    nc.tensor.matmul(
+                        banks[e][:],
+                        weights[e][:, kb, :],
+                        blocks[kb][:].indirect(offsets[:, e * QC : (e + 1) * QC]),
+                        start=(kb == 0),
+                        stop=(kb == KB - 1),
+                    )
+            for e in turn:
+                result = held.tile([P, Q], F32, name=f"result{e}")
+                nc.vector.tensor_scalar(result[:], banks[e][:], bias[:, 0:1], 0.0, op0=ADD, op1=MAX)
+                nc.sync.dma_start(out[:, e * Q : (e + 1) * Q], result[:])

@@ -38,9 +38,9 @@ def tile_gather_matmul_kernel(tc, table, w, b, offs, out):
 
         turns = ((0, 1), (2,), (3,))
 
-        nc.sync.dma_start(offsets[:], offs)
-        load_block(nc.sync, 0)
         load_weights(nc.sync, 0)
+        load_block(nc.sync, 0)
+        nc.sync.dma_start(offsets[:], offs)
         load_weights(nc.sync, 1)
         load_block(nc.sync, 1)
         load_block(nc.sync, 2)

@@ -26,8 +26,10 @@ def tile_gather_matmul_kernel(tc, table, w, b, offs, out):
     ):
         table_blocks = table.rearrange("(p kb) s -> kb p s", kb=KB)
         offsets = held.tile([P, N // 16], U16, name="offsets")
-        blocks = [held.tile([P, S], BF16, name=f"block{kb}") for kb in range(KB)]
-        weights = [held.tile([P, KB, M], BF16, name=f"weights{e}") for e in range(E)]
+        blocks = [held.tile([P, S], BF16, name=f"block{kb}", align_bytes=2 * S) for kb in range(KB)]
+        weights = [
+            held.tile([P, KB, M], BF16, name=f"weights{e}", align_bytes=2 * KB * M) for e in range(E)
+        ]
         bias = held.tile([P, 1], F32, name="bias")
 
         def load_block(queue, kb):
@@ -67,6 +69,6 @@ def tile_gather_matmul_kernel(tc, table, w, b, offs, out):
                         stop=(kb == KB - 1),
                     )
             for e in turn:
-                result = held.tile([P, Q], F32, name=f"result{e}")
+                result = held.tile([P, Q], F32, name=f"result{e}", align_bytes=4 * Q)
                 nc.vector.tensor_scalar(result[:], banks[e][:], bias[:, 0:1], 0.0, op0=ADD, op1=MAX)
                 nc.sync.dma_start(out[:, e * Q : (e + 1) * Q], result[:])

@@ -48,8 +48,8 @@ def tile_gather_matmul_kernel(tc, table, w, b, offs, out):
         load_block(nc.sync, 2)
         load_block(nc.sync, 3)
         load_weights(nc.sync, 2)
-        load_weights(nc.sync, 3)
         nc.sync.dma_start(bias[:], b)
+        load_weights(nc.sync, 3)
 
         zeros = held.tile([P, P], BF16, name="zeros")
         nc.vector.memset(zeros[:], 0.0)

import concourse.mybir as mybir

BF16, F32, U16 = mybir.dt.bfloat16, mybir.dt.float32, mybir.dt.uint16
ADD, MAX = mybir.AluOpType.add, mybir.AluOpType.max

P = 128
S = 256
K = 512
M = 128
E = 4
Q = 128
N = E * Q
KB = K // P
QC = Q // 16

WARM_MATMULS = 14

FLOPS = 2 * K * M * N


def tile_gather_matmul_kernel(tc, table, w, b, offs, out):
    nc = tc.nc
    with (
        tc.tile_pool(name="held", bufs=1) as held,
        tc.psum_pool(name="psum", bufs=1) as psum,
    ):
        table_blocks = table.rearrange("(p kb) s -> kb p s", kb=KB)
        offsets = held.tile([P, N // 16], U16, name="offsets")
        blocks = [held.tile([P, S], BF16, name=f"block{kb}", align_bytes=2 * S) for kb in range(KB)]
        weights = [
            held.tile([P, KB, M], BF16, name=f"weights{e}", align_bytes=2 * KB * M) for e in range(E)
        ]
        bias = held.tile([P, 1], F32, name="bias")

        def load_block(queue, kb):
            queue.dma_start(blocks[kb][:], table_blocks[kb])

        def load_weights(queue, e):
            queue.dma_start(weights[e][:], w[e].rearrange("(p kb) m -> p kb m", kb=KB))

        turns = ((0, 1), (2,), (3,))

        load_weights(nc.sync, 0)
        load_block(nc.sync, 0)
        nc.sync.dma_start(offsets[:], offs)
        load_weights(nc.sync, 1)
        load_block(nc.sync, 1)
        load_block(nc.sync, 2)
        load_block(nc.sync, 3)
        load_weights(nc.sync, 2)
        nc.sync.dma_start(bias[:], b)
        load_weights(nc.sync, 3)

        zeros = held.tile([P, P], BF16, name="zeros")
        nc.vector.memset(zeros[:], 0.0)
        unread = psum.tile([P, P], F32, name="unread")
        for i in range(WARM_MATMULS):
            nc.tensor.matmul(unread[:], zeros[:], zeros[:], start=True, stop=True)

        banks = [psum.tile([P, Q], F32, name=f"bank{e}") for e in range(E)]
        for turn in turns:
            for kb in range(KB):
                for e in turn:
                    nc.tensor.matmul(
                        banks[e][:],
                        weights[e][:, kb, :],
                        blocks[kb][:].indirect(offsets[:, e * QC : (e + 1) * QC]),
                        start=(kb == 0),
                        stop=(kb == KB - 1),
                    )
            for e in turn:
                result = held.tile([P, Q], F32, name=f"result{e}", align_bytes=4 * Q)
                nc.vector.tensor_scalar(result[:], banks[e][:], bias[:, 0:1], 0.0, op0=ADD, op1=MAX)
                nc.sync.dma_start(out[:, e * Q : (e + 1) * Q], result[:])
